import numpy as np
import ml_dtypes


def mxq(x, axis, fmt="e4m3"):
    dtype, down = {"e4m3": (ml_dtypes.float8_e4m3fn, 7), "e5m2": (ml_dtypes.float8_e5m2, 14)}[fmt]
    v = np.moveaxis(np.asarray(x, np.float32).astype(ml_dtypes.bfloat16).astype(np.float64), axis, -1)
    blocks = v.reshape(v.shape[:-1] + (-1, 32))
    amax = np.abs(blocks).max(-1, keepdims=True)
    byte = np.maximum(np.where(amax > 0, np.frexp(amax)[1] - 1 + 127, 0) - down, 1)
    scale = np.exp2(byte - 127.0)
    codes = (blocks / scale).astype(np.float32).astype(dtype).astype(np.float64)
    return np.moveaxis((codes * scale).reshape(v.shape), -1, axis)


WIDE = False


def mx_kscale(k):
    if not WIDE:
        return np.ones(k)
    levels = np.array([10, -10, 5, -5, 0])
    if k % 512:
        return np.exp2(np.random.permutation(np.resize(levels, k // 32))).repeat(32)
    a = np.empty((k // 512, 16))
    for p in range(k // 512):
        a[p, :8] = np.random.permutation(np.resize(levels, 8))
        for g in range(8):
            far = levels[np.abs(levels - a[p, g]) >= 10]
            a[p, g + 8] = far[np.random.randint(len(far))]
    return np.exp2(a.ravel()).repeat(32)


def f64(x):
    return np.asarray(x).astype(np.float64)


def striped(idx):
    return np.tile(np.asarray(idx).reshape(-1, 16).T, (8, 1)).astype(np.uint16)


def unstriped(offs):
    return offs[:16].T.reshape(-1).astype(np.int64)


E2M1 = np.array([0.0, 0.5, 1.0, 1.5, 2.0, 3.0, 4.0, 6.0, -0.0, -0.5, -1.0, -1.5, -2.0, -3.0, -4.0, -6.0])


def pack_weight(w, fmt):
    k, n = w.shape
    w = f64(np.asarray(w, np.float32).astype(ml_dtypes.bfloat16)).reshape(k // 32, 32, n)
    amax = np.abs(w).max(1)
    if fmt == "e4m3":
        byte = np.frexp(amax)[1] - 1 + 127 - 7
    else:
        mant, ex = np.frexp(amax / 6.0)
        byte = np.where(mant > 0.5, ex, ex - 1) + 127
    byte = np.clip(np.where(amax > 0, byte, 1), 1, 254)
    scaled = (w * np.exp2(127.0 - byte)[:, None, :]).reshape(k, n).astype(np.float32)
    by_word = np.ascontiguousarray(scaled.reshape(k // 512, 128, 4, n).transpose(0, 1, 3, 2))
    if fmt == "e4m3":
        words = by_word.astype(ml_dtypes.float8_e4m3fn).view(np.uint8)
    else:
        c = by_word.astype(ml_dtypes.float4_e2m1fn).view(np.uint8) & 0xF
        words = (c[..., 0::2] | (c[..., 1::2] << 4)).reshape(k // 512, 128, 2 * n)
    return np.ascontiguousarray(words), np.ascontiguousarray(byte.astype(np.uint8).reshape(k // 512, 16, n))


def unpack_weight(words, scales, fmt):
    g, _, n = scales.shape
    words = np.ascontiguousarray(words).reshape(g, 128, n, -1)
    if fmt == "e4m3":
        vals = words.view(ml_dtypes.float8_e4m3fn).astype(np.float64)
    else:
        nib = np.empty((g, 128, n, 4), np.uint8)
        nib[..., 0::2] = words & 0xF
        nib[..., 1::2] = words >> 4
        vals = E2M1[nib]
    vals = vals * np.repeat(np.exp2(scales.astype(np.float64) - 127.0), 8, axis=1)[..., None]
    return vals.transpose(0, 1, 3, 2).reshape(g * 512, n)


def sigmoid(v):
    return 1.0 / (1.0 + np.exp(-v))


K, R, F, T, J, G = 512, 128, 512, 2048, 512, 64


def setup_inputs():
    n = np.random.standard_normal
    idx = np.random.permutation(T)[:J]
    fk = mx_kscale(K)
    ff = mx_kscale(F)
    tabp = pack_weight(n((K, T)) / fk[:, None], "e2m1")
    return {
        "tab_words": tabp[0],
        "tab_scales": tabp[1],
        "w1": (n((K, R)) * 1 / np.sqrt(K) * fk[:, None]).astype(np.float32),
        "steep": (np.random.uniform(1.0, 4.0, (R, 1))).astype(np.float32),
        "wo": (n((F, R)) * 1 / np.sqrt(F) * ff[:, None]).astype(np.float32),
        "dy": (n((F, G)) / ff[:, None]).astype(np.float32),
        "og": (np.random.uniform(0.3, 1.0, (R, 1))).astype(np.float32),
        "base": (0.3 * n((R, J))).astype(np.float32),
        "offs": striped(idx),
    }


def reference(tab_words, tab_scales, w1, steep, wo, dy, og, base, offs):
    idx = unstriped(offs)
    tabu = unpack_weight(tab_words, tab_scales, "e2m1")
    w1q = mxq(f64(w1), 0, "e4m3")
    tabidxg = tabu[:, idx]
    a = w1q.T @ tabidxg
    h1 = np.tanh(a)
    p = sigmoid(a * f64(steep))
    z = p.reshape(R, G, J // G).sum(axis=2)
    woq = mxq(f64(wo), 0, "e4m3")
    dyq = mxq(f64(dy), 0, "e4m3")
    c0 = woq.T @ dyq
    e1 = c0 / z
    r1 = np.repeat(e1, J // G, axis=1)
    dz = c0 * (p * h1).reshape(R, G, J // G).sum(axis=2) / np.square(z) * (-1.0)
    r2 = np.repeat(dz, J // G, axis=1)
    dp = r1 * h1 + r2
    dh1 = r1 * p
    da = dp * p * (1.0 - p) * f64(steep) + dh1 * (1.0 - np.square(h1))
    hda = da * 2.0
    hdh1 = hda * (1.0 - np.square(h1))
    hdp = hda * f64(steep) * (1.0 - p) * p
    hdz = hdp.reshape(R, G, J // G).sum(axis=2)
    e51 = hdz * (-1.0) / np.square(z) * c0
    r51 = np.repeat(e51, J // G, axis=1)
    hr1 = hdh1 * p + hdp * h1
    he1 = hr1.reshape(R, G, J // G).sum(axis=2)
    hz = hdz * (-1.0) * c0 * (p * h1).reshape(R, G, J // G).sum(axis=2) / np.square(np.square(z)) * (-1.0) * z * 2.0 - he1 * c0 / np.square(z)
    r52 = np.repeat(hz, J // G, axis=1)
    hp = hda * f64(steep) * (1.0 - p) * dp + hdh1 * r1 + r51 * h1 + r52 - hda * f64(steep) * dp * p
    hh1 = hda * dh1 * (-1.0) * h1 * 2.0 + hdp * r1 + r51 * p
    ha = hp * p * (1.0 - p) * f64(steep) + hh1 * (1.0 - np.square(h1))
    y = ha * f64(og) + f64(base)
    return y

@@ -1,0 +1,236 @@
+import math
+from contextlib import ExitStack
+
+import concourse.mybir as mybir
+
+K, R, F, T, J, G = 512, 128, 512, 2048, 512, 64
+FLOPS = 2 * K * R * J + 2 * F * R * G
+
+F32 = mybir.dt.float32
+BF16 = mybir.dt.bfloat16
+I32 = mybir.dt.int32
+U32 = mybir.dt.uint32
+U16 = mybir.dt.uint16
+U8 = mybir.dt.uint8
+FP8X4 = mybir.dt.float8_e4m3fn_x4
+FP4X4 = mybir.dt.float4_e2m1fn_x4
+ACT = mybir.ActivationFunctionType
+ALU = mybir.AluOpType
+AXIS_X = mybir.AxisListType.X
+
+P = 128
+PACK = 4
+GROUP = J // G
+HALVES = 2
+HJ = J // HALVES
+HG = G // HALVES
+WORDS_FIRST = T - T // 8
+
+
+def grouped(ap):
+    return ap.rearrange("p (g i) -> p g i", i=GROUP)
+
+
+def spread(ap):
+    return ap.rearrange("p (g o) -> p g o", o=1).to_broadcast([P, HG, GROUP])
+
+
+def tile_attend_gpgroupvote_kernel(tc, tab_words, tab_scales, w1, steep, wo, dy, og, base, offs, out):
+    nc = tc.nc
+    with ExitStack() as ctx:
+        keep = ctx.enter_context(tc.tile_pool(name="keep", bufs=1))
+        reuse = ctx.enter_context(tc.tile_pool(name="reuse", bufs=1))
+        psum = ctx.enter_context(tc.psum_pool(name="psum", bufs=1))
+
+        def wide(name, h):
+            return keep.tile([P, HJ], F32, name=f"{name}{h}", align_bytes=64)
+
+        def narrow(name, h):
+            return keep.tile([P, HG], F32, name=f"{name}{h}", align_bytes=64)
+
+        halves = range(HALVES)
+
+        offsets = keep.tile([P, J // 16], U16)
+        nc.sync.dma_start(offsets[:], offs)
+
+        scale_window = keep.tile([P, T], U8, align_bytes=64)
+        nc.vector.memset(scale_window[:].bitcast(I32), 0)
+        warm_in = keep.tile([P, 1], F32)
+        nc.vector.memset(warm_in[:], 0.0)
+        for q in range(4):
+            nc.scalar.dma_start(
+                out=scale_window[32 * q : 32 * q + 4, :].bitcast(I32),
+                in_=tab_scales[0, 4 * q : 4 * q + 4, :].bitcast(I32),
+            )
+        word_window = keep.tile([P, T], U16, align_bytes=64)
+        words_in = tab_words[0].bitcast(I32)
+        split = WORDS_FIRST // 2
+        nc.scalar.dma_start(out=word_window[:].bitcast(I32)[:, split:], in_=words_in[:, split:])
+        warm_out = keep.tile([P, 1], F32)
+        nc.scalar.activation(warm_out[:], warm_in[:], ACT.Sigmoid)
+
+        w1_raw = keep.tile([P, PACK, R], F32, tag="stage", align_bytes=64)
+        nc.sync.dma_start(out=w1_raw[:], in_=w1.rearrange("(p t) r -> p t r", t=PACK))
+        nc.sync.dma_start(out=word_window[:].bitcast(I32)[:, :split], in_=words_in[:, :split])
+
+        s = keep.tile([P, 1], F32)
+        nc.gpsimd.dma_start(out=s[:], in_=steep)
+        gain = keep.tile([P, 1], F32)
+        nc.gpsimd.dma_start(out=gain[:], in_=og)
+        s_twice = keep.tile([P, 1], F32)
+        nc.gpsimd.tensor_scalar(s_twice[:], s[:], 2.0, 0.0, ALU.mult, ALU.add)
+
+        def interleave(dst, src):
+            nc.scalar.copy(
+                out=dst.rearrange("p (c i) t -> p c t i", i=4),
+                in_=src.rearrange("p t (c i) -> p c t i", i=4),
+            )
+
+        def quantise(name, values, width):
+            codes = keep.tile([P, width], U32, name=f"{name}_codes", align_bytes=64)
+            scales = keep.tile([P, width], U8, name=f"{name}_scales", align_bytes=64)
+            nc.vector.quantize_mx(out=codes[:].bitcast(FP8X4), scales=scales[:], in_=values.rearrange("p c t -> p (c t)"))
+            return codes, scales
+
+        w1_bf = reuse.tile([P, R, PACK], BF16, align_bytes=64, offset=0)
+        interleave(w1_bf[:], w1_raw[:])
+
+        lists = [offsets[:, h * (HJ // 16) : (h + 1) * (HJ // 16)] for h in halves]
+        tab_s0 = keep.tile([P, HJ], U8, align_bytes=64)
+        tab_w0 = keep.tile([P, HJ], U16, align_bytes=64)
+        nc.vector.tensor_copy(tab_s0[:], scale_window[:].indirect(lists[0]))
+        nc.vector.tensor_copy(tab_w0[:], word_window[:].indirect(lists[0]))
+        w1_codes, w1_scales = quantise("w1", w1_bf[:], R)
+        tab_s1 = reuse.tile([P, HJ], U8, align_bytes=64, offset=0)
+        tab_w1 = reuse.tile([P, HJ], U16, align_bytes=64, offset=HJ)
+        nc.vector.tensor_copy(tab_s1[:], scale_window[:].indirect(lists[1]))
+        nc.vector.tensor_copy(tab_w1[:], word_window[:].indirect(lists[1]))
+        a = [psum.tile([P, HJ], F32, name=f"a{h}") for h in halves]
+        for h, (tab_w, tab_s) in enumerate(((tab_w0, tab_s0), (tab_w1, tab_s1))):
+            nc.tensor.matmul_mx(
+                out=a[h][:],
+                lhsT=w1_codes[:].bitcast(FP8X4),
+                lhsT_scale=w1_scales[:],
+                rhs=tab_w[:].bitcast(FP4X4),
+                rhs_scale=tab_s[:],
+                start=True,
+                stop=True,
+            )
+
+        p = [wide("p", h) for h in halves]
+        h1 = [wide("h1", h) for h in halves]
+        h_sq = [wide("h_sq", h) for h in halves]
+        slope = [wide("slope", h) for h in halves]
+        ph = [wide("ph", h) for h in halves]
+        z = [narrow("z", h) for h in halves]
+        rz = [narrow("rz", h) for h in halves]
+        ph_sum = [narrow("ph_sum", h) for h in halves]
+        mean = [narrow("mean", h) for h in halves]
+        s_rz = [narrow("s_rz", h) for h in halves]
+        for h in halves:
+            nc.scalar.activation(p[h][:], a[h][:], ACT.Sigmoid, scale=s[:])
+            nc.scalar.activation(h1[h][:], a[h][:], ACT.Tanh)
+            nc.vector.tensor_reduce(z[h][:], grouped(p[h][:]), AXIS_X, ALU.add)
+            nc.vector.tensor_tensor(ph[h][:], p[h][:], h1[h][:], ALU.mult)
+            nc.vector.reciprocal(rz[h][:], z[h][:])
+        for h in halves:
+            nc.scalar.activation(h_sq[h][:], h1[h][:], ACT.Square)
+            nc.vector.tensor_reduce(ph_sum[h][:], grouped(ph[h][:]), AXIS_X, ALU.add)
+        for h in halves:
+            nc.scalar.activation(slope[h][:], h1[h][:], ACT.Identity, bias=s[:], scale=-2.0)
+            nc.scalar.activation(s_rz[h][:], rz[h][:], ACT.Copy, scale=s[:])
+
+        last_raw = keep.tile([P, PACK * (R + G)], F32, tag="stage", align_bytes=64)
+        wo_raw = last_raw[:, : PACK * R].rearrange("p (t r) -> p t r", t=PACK)
+        dy_raw = last_raw[:, PACK * R :].rearrange("p (t g) -> p t g", t=PACK)
+        nc.sync.dma_start(out=wo_raw, in_=wo.rearrange("(p t) r -> p t r", t=PACK))
+        nc.sync.dma_start(out=dy_raw, in_=dy.rearrange("(p t) g -> p t g", t=PACK))
+        wo_bf = keep.tile([P, R, PACK], BF16, align_bytes=64)
+        dy_bf = keep.tile([P, G, PACK], BF16, align_bytes=64)
+        interleave(wo_bf[:], wo_raw)
+        interleave(dy_bf[:], dy_raw)
+        base_sb = keep.tile([P, J], F32, tag="stage", align_bytes=64)
+        nc.sync.dma_start(out=base_sb[:], in_=base)
+
+        nq = [wide("nq", h) for h in halves]
+        npu = [wide("npu", h) for h in halves]
+        d = [wide("d", h) for h in halves]
+        ndq = [wide("ndq", h) for h in halves]
+        na = [wide("na", h) for h in halves]
+        a_sq = [wide("a_sq", h) for h in halves]
+        tilt = [wide("tilt", h) for h in halves]
+        aq = [wide("aq", h) for h in halves]
+        for h in halves:
+            nc.vector.tensor_tensor(mean[h][:], ph_sum[h][:], rz[h][:], ALU.mult)
+        for h in halves:
+            nc.vector.scalar_tensor_tensor(nq[h][:], p[h][:], 1.0, p[h][:], ALU.subtract, ALU.mult)
+        for h in halves:
+            nc.vector.tensor_tensor(grouped(d[h][:]), grouped(h1[h][:]), spread(mean[h][:]), ALU.subtract)
+        for h in halves:
+            nc.vector.scalar_tensor_tensor(npu[h][:], h_sq[h][:], 1.0, p[h][:], ALU.subtract, ALU.mult)
+        for h in halves:
+            nc.vector.scalar_tensor_tensor(ndq[h][:], d[h][:], s[:], nq[h][:], ALU.mult, ALU.mult)
+        for h in halves:
+            nc.vector.tensor_tensor(na[h][:], ndq[h][:], npu[h][:], ALU.add)
+            nc.scalar.activation(a_sq[h][:], na[h][:], ACT.Square)
+        for h in halves:
+            nc.vector.tensor_tensor(aq[h][:], na[h][:], nq[h][:], ALU.mult)
+        for h in halves:
+            nc.vector.scalar_tensor_tensor(tilt[h][:], p[h][:], 0.5, na[h][:], ALU.subtract, ALU.mult)
+
+        bend = [keep.tile([P, HJ], F32, name=f"bend{h}", tag=f"p{h}", align_bytes=64) for h in halves]
+        for h in halves:
+            nc.gpsimd.tensor_tensor(bend[h][:], slope[h][:], npu[h][:], ALU.mult)
+
+        sums = [keep.tile([P, 2, HG], F32, name=f"sums{h}", align_bytes=64) for h in halves]
+        coef = [keep.tile([P, 2, HG], F32, name=f"coef{h}", align_bytes=64) for h in halves]
+        for h in halves:
+            nc.vector.tensor_reduce(sums[h][:, 1, :], grouped(a_sq[h][:]), AXIS_X, ALU.add)
+        for h in halves:
+            nc.vector.tensor_reduce(sums[h][:, 0, :], grouped(aq[h][:]), AXIS_X, ALU.add)
+
+        wo_codes, wo_scales = quantise("wo", wo_bf[:], R)
+        dy_codes, dy_scales = quantise("dy", dy_bf[:], G)
+        c0 = psum.tile([P, G], F32)
+        nc.tensor.matmul_mx(
+            out=c0[:],
+            lhsT=wo_codes[:].bitcast(FP8X4),
+            lhsT_scale=wo_scales[:],
+            rhs=dy_codes[:].bitcast(FP8X4),
+            rhs_scale=dy_scales[:],
+            start=True,
+            stop=True,
+        )
+
+        curve = [wide("curve", h) for h in halves]
+        e = [narrow("e", h) for h in halves]
+        weight = [narrow("weight", h) for h in halves]
+        for h in halves:
+            nc.vector.tensor_tensor(
+                coef[h][:], sums[h][:], s_rz[h][:].rearrange("p (o g) -> p o g", o=1).to_broadcast([P, 2, HG]), ALU.mult
+            )
+        for h in halves:
+            nc.vector.scalar_tensor_tensor(curve[h][:], tilt[h][:], s_twice[:], bend[h][:], ALU.mult, ALU.subtract)
+        for h in halves:
+            nc.vector.tensor_tensor(e[h][:], c0[:, h * HG : (h + 1) * HG], rz[h][:], ALU.mult)
+            nc.scalar.activation(weight[h][:], e[h][:], ACT.Square, scale=math.sqrt(2.0))
+        t0 = [wide("t0", h) for h in halves]
+        t1 = [wide("t1", h) for h in halves]
+        t2 = [wide("t2", h) for h in halves]
+        t3 = [wide("t3", h) for h in halves]
+        t4 = [wide("t4", h) for h in halves]
+        result = [wide("result", h) for h in halves]
+        for h in halves:
+            nc.vector.tensor_tensor(grouped(t0[h][:]), grouped(curve[h][:]), spread(coef[h][:, 0, :]), ALU.subtract)
+        for h in halves:
+            nc.vector.tensor_tensor(grouped(t2[h][:]), grouped(nq[h][:]), spread(coef[h][:, 1, :]), ALU.mult)
+        for h in halves:
+            nc.vector.tensor_tensor(t1[h][:], na[h][:], t0[h][:], ALU.mult)
+        for h in halves:
+            nc.vector.tensor_tensor(t3[h][:], t2[h][:], t1[h][:], ALU.subtract)
+        for h in halves:
+            nc.vector.tensor_tensor(grouped(t4[h][:]), grouped(t3[h][:]), spread(weight[h][:]), ALU.mult)
+        for h in halves:
+            cols = slice(h * HJ, (h + 1) * HJ)
+            nc.vector.scalar_tensor_tensor(result[h][:], t4[h][:], gain[:], base_sb[:, cols], ALU.mult, ALU.add)
+            nc.sync.dma_start(out=out[:, cols], in_=result[h][:])

@@ -1,4 +1,3 @@
-import math
 from contextlib import ExitStack
 
 import concourse.mybir as mybir
@@ -24,7 +23,6 @@ GROUP = J // G
 HALVES = 2
 HJ = J // HALVES
 HG = G // HALVES
-WORDS_FIRST = T - T // 8
 
 
 def grouped(ap):
@@ -39,46 +37,36 @@ def tile_attend_gpgroupvote_kernel(tc, tab_words, tab_scales, w1, steep, wo, dy,
     nc = tc.nc
     with ExitStack() as ctx:
         keep = ctx.enter_context(tc.tile_pool(name="keep", bufs=1))
-        reuse = ctx.enter_context(tc.tile_pool(name="reuse", bufs=1))
         psum = ctx.enter_context(tc.psum_pool(name="psum", bufs=1))
-
-        def wide(name, h):
-            return keep.tile([P, HJ], F32, name=f"{name}{h}", align_bytes=64)
-
-        def narrow(name, h):
-            return keep.tile([P, HG], F32, name=f"{name}{h}", align_bytes=64)
 
         halves = range(HALVES)
 
+        def per_half(name, width):
+            return [keep.tile([P, width], F32, name=f"{name}{h}", align_bytes=64) for h in halves]
+
         offsets = keep.tile([P, J // 16], U16)
         nc.sync.dma_start(offsets[:], offs)
+        s = keep.tile([P, 1], F32)
+        nc.scalar.dma_start(out=s[:], in_=steep)
+        w1_raw = keep.tile([P, PACK, R], F32, tag="stage", align_bytes=64)
+        nc.sync.dma_start(out=w1_raw[:], in_=w1.rearrange("(p t) r -> p t r", t=PACK))
 
         scale_window = keep.tile([P, T], U8, align_bytes=64)
         nc.vector.memset(scale_window[:].bitcast(I32), 0)
-        warm_in = keep.tile([P, 1], F32)
-        nc.vector.memset(warm_in[:], 0.0)
         for q in range(4):
-            nc.scalar.dma_start(
+            nc.sync.dma_start(
                 out=scale_window[32 * q : 32 * q + 4, :].bitcast(I32),
                 in_=tab_scales[0, 4 * q : 4 * q + 4, :].bitcast(I32),
             )
         word_window = keep.tile([P, T], U16, align_bytes=64)
-        words_in = tab_words[0].bitcast(I32)
-        split = WORDS_FIRST // 2
-        nc.scalar.dma_start(out=word_window[:].bitcast(I32)[:, split:], in_=words_in[:, split:])
+        nc.sync.dma_start(out=word_window[:].bitcast(I32), in_=tab_words[0].bitcast(I32))
+        gain = keep.tile([P, 1], F32)
+        nc.sync.dma_start(out=gain[:], in_=og)
+
+        warm_in = keep.tile([P, 1], F32)
+        nc.gpsimd.memset(warm_in[:], 0.0)
         warm_out = keep.tile([P, 1], F32)
         nc.scalar.activation(warm_out[:], warm_in[:], ACT.Sigmoid)
-
-        w1_raw = keep.tile([P, PACK, R], F32, tag="stage", align_bytes=64)
-        nc.sync.dma_start(out=w1_raw[:], in_=w1.rearrange("(p t) r -> p t r", t=PACK))
-        nc.sync.dma_start(out=word_window[:].bitcast(I32)[:, :split], in_=words_in[:, :split])
-
-        s = keep.tile([P, 1], F32)
-        nc.gpsimd.dma_start(out=s[:], in_=steep)
-        gain = keep.tile([P, 1], F32)
-        nc.gpsimd.dma_start(out=gain[:], in_=og)
-        s_twice = keep.tile([P, 1], F32)
-        nc.gpsimd.tensor_scalar(s_twice[:], s[:], 2.0, 0.0, ALU.mult, ALU.add)
 
         def interleave(dst, src):
             nc.scalar.copy(
@@ -92,53 +80,44 @@ def tile_attend_gpgroupvote_kernel(tc, tab_words, tab_scales, w1, steep, wo, dy,
             nc.vector.quantize_mx(out=codes[:].bitcast(FP8X4), scales=scales[:], in_=values.rearrange("p c t -> p (c t)"))
             return codes, scales
 
-        w1_bf = reuse.tile([P, R, PACK], BF16, align_bytes=64, offset=0)
+        w1_bf = keep.tile([P, R, PACK], BF16, align_bytes=64)
         interleave(w1_bf[:], w1_raw[:])
+        s_half = keep.tile([P, 1], F32)
+        nc.gpsimd.tensor_scalar(s_half[:], s[:], 0.5, 0.0, ALU.mult, ALU.add)
+        neg_gain = keep.tile([P, 1], F32)
+        nc.gpsimd.tensor_scalar(neg_gain[:], gain[:], -1.0, 0.0, ALU.mult, ALU.add)
 
         lists = [offsets[:, h * (HJ // 16) : (h + 1) * (HJ // 16)] for h in halves]
-        tab_s0 = keep.tile([P, HJ], U8, align_bytes=64)
-        tab_w0 = keep.tile([P, HJ], U16, align_bytes=64)
-        nc.vector.tensor_copy(tab_s0[:], scale_window[:].indirect(lists[0]))
-        nc.vector.tensor_copy(tab_w0[:], word_window[:].indirect(lists[0]))
+        tab_s = [keep.tile([P, HJ], U8, name=f"tab_s{h}", align_bytes=64) for h in halves]
+        tab_w = [keep.tile([P, HJ], U16, name=f"tab_w{h}", align_bytes=64) for h in halves]
+        for h in halves:
+            nc.vector.tensor_copy(tab_s[h][:], scale_window[:].indirect(lists[h]))
         w1_codes, w1_scales = quantise("w1", w1_bf[:], R)
-        tab_s1 = reuse.tile([P, HJ], U8, align_bytes=64, offset=0)
-        tab_w1 = reuse.tile([P, HJ], U16, align_bytes=64, offset=HJ)
-        nc.vector.tensor_copy(tab_s1[:], scale_window[:].indirect(lists[1]))
-        nc.vector.tensor_copy(tab_w1[:], word_window[:].indirect(lists[1]))
         a = [psum.tile([P, HJ], F32, name=f"a{h}") for h in halves]
-        for h, (tab_w, tab_s) in enumerate(((tab_w0, tab_s0), (tab_w1, tab_s1))):
+        for h in halves:
+            nc.vector.tensor_copy(tab_w[h][:], word_window[:].indirect(lists[h]))
             nc.tensor.matmul_mx(
                 out=a[h][:],
                 lhsT=w1_codes[:].bitcast(FP8X4),
                 lhsT_scale=w1_scales[:],
-                rhs=tab_w[:].bitcast(FP4X4),
-                rhs_scale=tab_s[:],
+                rhs=tab_w[h][:].bitcast(FP4X4),
+                rhs_scale=tab_s[h][:],
                 start=True,
                 stop=True,
             )
 
-        p = [wide("p", h) for h in halves]
-        h1 = [wide("h1", h) for h in halves]
-        h_sq = [wide("h_sq", h) for h in halves]
-        slope = [wide("slope", h) for h in halves]
-        ph = [wide("ph", h) for h in halves]
-        z = [narrow("z", h) for h in halves]
-        rz = [narrow("rz", h) for h in halves]
-        ph_sum = [narrow("ph_sum", h) for h in halves]
-        mean = [narrow("mean", h) for h in halves]
-        s_rz = [narrow("s_rz", h) for h in halves]
+        p, h1, h_sq, ph = (per_half(name, HJ) for name in ("p", "h1", "h_sq", "ph"))
+        nq, npu, d, ndq, na = (per_half(name, HJ) for name in ("nq", "npu", "d", "ndq", "na"))
+        a_sq, tilt, aq, bend, curve = (per_half(name, HJ) for name in ("a_sq", "tilt", "aq", "bend", "curve"))
+        t0, t1, t2, shifted, result, wa = (per_half(name, HJ) for name in ("t0", "t1", "t2", "shifted", "result", "wa"))
+        z, rz, ph_sum, mean, e, weight = (per_half(name, HG) for name in ("z", "rz", "ph_sum", "mean", "e", "weight"))
+        sums, factor, coef = (per_half(name, 2 * HG) for name in ("sums", "factor", "coef"))
+
         for h in halves:
             nc.scalar.activation(p[h][:], a[h][:], ACT.Sigmoid, scale=s[:])
             nc.scalar.activation(h1[h][:], a[h][:], ACT.Tanh)
-            nc.vector.tensor_reduce(z[h][:], grouped(p[h][:]), AXIS_X, ALU.add)
-            nc.vector.tensor_tensor(ph[h][:], p[h][:], h1[h][:], ALU.mult)
-            nc.vector.reciprocal(rz[h][:], z[h][:])
         for h in halves:
             nc.scalar.activation(h_sq[h][:], h1[h][:], ACT.Square)
-            nc.vector.tensor_reduce(ph_sum[h][:], grouped(ph[h][:]), AXIS_X, ALU.add)
-        for h in halves:
-            nc.scalar.activation(slope[h][:], h1[h][:], ACT.Identity, bias=s[:], scale=-2.0)
-            nc.scalar.activation(s_rz[h][:], rz[h][:], ACT.Copy, scale=s[:])
 
         last_raw = keep.tile([P, PACK * (R + G)], F32, tag="stage", align_bytes=64)
         wo_raw = last_raw[:, : PACK * R].rearrange("p (t r) -> p t r", t=PACK)
@@ -151,86 +130,152 @@ def tile_attend_gpgroupvote_kernel(tc, tab_words, tab_scales, w1, steep, wo, dy,
         interleave(dy_bf[:], dy_raw)
         base_sb = keep.tile([P, J], F32, tag="stage", align_bytes=64)
         nc.sync.dma_start(out=base_sb[:], in_=base)
+        c0 = psum.tile([P, G], F32)
 
-        nq = [wide("nq", h) for h in halves]
-        npu = [wide("npu", h) for h in halves]
-        d = [wide("d", h) for h in halves]
-        ndq = [wide("ndq", h) for h in halves]
-        na = [wide("na", h) for h in halves]
-        a_sq = [wide("a_sq", h) for h in halves]
-        tilt = [wide("tilt", h) for h in halves]
-        aq = [wide("aq", h) for h in halves]
-        for h in halves:
-            nc.vector.tensor_tensor(mean[h][:], ph_sum[h][:], rz[h][:], ALU.mult)
-        for h in halves:
+        def step_z(h):
+            nc.vector.tensor_reduce(z[h][:], grouped(p[h][:]), AXIS_X, ALU.add)
+
+        def step_ph(h):
+            nc.vector.tensor_tensor(ph[h][:], p[h][:], h1[h][:], ALU.mult)
+
+        def step_nq(h):
             nc.vector.scalar_tensor_tensor(nq[h][:], p[h][:], 1.0, p[h][:], ALU.subtract, ALU.mult)
-        for h in halves:
+
+        def step_rz(h):
+            nc.vector.reciprocal(rz[h][:], z[h][:])
+            nc.scalar.activation(factor[h][:, :HG], rz[h][:], ACT.Copy, scale=s_half[:])
+
+        def step_ph_sum(h):
+            nc.vector.tensor_reduce(ph_sum[h][:], grouped(ph[h][:]), AXIS_X, ALU.add)
+
+        def step_mean(h):
+            nc.vector.tensor_tensor(mean[h][:], ph_sum[h][:], rz[h][:], ALU.mult)
+
+        def step_d(h):
             nc.vector.tensor_tensor(grouped(d[h][:]), grouped(h1[h][:]), spread(mean[h][:]), ALU.subtract)
-        for h in halves:
+
+        def step_npu(h):
             nc.vector.scalar_tensor_tensor(npu[h][:], h_sq[h][:], 1.0, p[h][:], ALU.subtract, ALU.mult)
-        for h in halves:
+
+        def step_ndq(h):
             nc.vector.scalar_tensor_tensor(ndq[h][:], d[h][:], s[:], nq[h][:], ALU.mult, ALU.mult)
-        for h in halves:
+
+        def step_na(h):
             nc.vector.tensor_tensor(na[h][:], ndq[h][:], npu[h][:], ALU.add)
             nc.scalar.activation(a_sq[h][:], na[h][:], ACT.Square)
-        for h in halves:
+
+        def step_wa(h):
+            for g in range(HG):
+                cols = slice(g * GROUP, (g + 1) * GROUP)
+                nc.scalar.activation(wa[h][:, cols], na[h][:, cols], ACT.Copy, scale=weight[h][:, g : g + 1])
+
+        def step_bend(h):
+            nc.vector.scalar_tensor_tensor(bend[h][:], h1[h][:], s_half[:], npu[h][:], ALU.subtract, ALU.mult)
+
+        def step_aq(h):
             nc.vector.tensor_tensor(aq[h][:], na[h][:], nq[h][:], ALU.mult)
-        for h in halves:
+
+        def step_tilt(h):
             nc.vector.scalar_tensor_tensor(tilt[h][:], p[h][:], 0.5, na[h][:], ALU.subtract, ALU.mult)
 
-        bend = [keep.tile([P, HJ], F32, name=f"bend{h}", tag=f"p{h}", align_bytes=64) for h in halves]
-        for h in halves:
-            nc.gpsimd.tensor_tensor(bend[h][:], slope[h][:], npu[h][:], ALU.mult)
+        def step_aq_sum(h):
+            nc.vector.tensor_reduce(sums[h][:, :HG], grouped(aq[h][:]), AXIS_X, ALU.add)
 
-        sums = [keep.tile([P, 2, HG], F32, name=f"sums{h}", align_bytes=64) for h in halves]
-        coef = [keep.tile([P, 2, HG], F32, name=f"coef{h}", align_bytes=64) for h in halves]
-        for h in halves:
-            nc.vector.tensor_reduce(sums[h][:, 1, :], grouped(a_sq[h][:]), AXIS_X, ALU.add)
-        for h in halves:
-            nc.vector.tensor_reduce(sums[h][:, 0, :], grouped(aq[h][:]), AXIS_X, ALU.add)
+        def step_a_sq_sum(h):
+            nc.vector.tensor_reduce(sums[h][:, HG:], grouped(a_sq[h][:]), AXIS_X, ALU.add)
 
-        wo_codes, wo_scales = quantise("wo", wo_bf[:], R)
-        dy_codes, dy_scales = quantise("dy", dy_bf[:], G)
-        c0 = psum.tile([P, G], F32)
-        nc.tensor.matmul_mx(
-            out=c0[:],
-            lhsT=wo_codes[:].bitcast(FP8X4),
-            lhsT_scale=wo_scales[:],
-            rhs=dy_codes[:].bitcast(FP8X4),
-            rhs_scale=dy_scales[:],
-            start=True,
-            stop=True,
-        )
+        def step_curve(h):
+            nc.vector.scalar_tensor_tensor(curve[h][:], tilt[h][:], s[:], bend[h][:], ALU.mult, ALU.add)
 
-        curve = [wide("curve", h) for h in halves]
-        e = [narrow("e", h) for h in halves]
-        weight = [narrow("weight", h) for h in halves]
-        for h in halves:
-            nc.vector.tensor_tensor(
-                coef[h][:], sums[h][:], s_rz[h][:].rearrange("p (o g) -> p o g", o=1).to_broadcast([P, 2, HG]), ALU.mult
+        def step_c0(h):
+            wo_codes, wo_scales = quantise("wo", wo_bf[:], R)
+            dy_codes, dy_scales = quantise("dy", dy_bf[:], G)
+            nc.tensor.matmul_mx(
+                out=c0[:],
+                lhsT=wo_codes[:].bitcast(FP8X4),
+                lhsT_scale=wo_scales[:],
+                rhs=dy_codes[:].bitcast(FP8X4),
+                rhs_scale=dy_scales[:],
+                start=True,
+                stop=True,
             )
-        for h in halves:
-            nc.vector.scalar_tensor_tensor(curve[h][:], tilt[h][:], s_twice[:], bend[h][:], ALU.mult, ALU.subtract)
-        for h in halves:
+
+        def step_e(h):
             nc.vector.tensor_tensor(e[h][:], c0[:, h * HG : (h + 1) * HG], rz[h][:], ALU.mult)
-            nc.scalar.activation(weight[h][:], e[h][:], ACT.Square, scale=math.sqrt(2.0))
-        t0 = [wide("t0", h) for h in halves]
-        t1 = [wide("t1", h) for h in halves]
-        t2 = [wide("t2", h) for h in halves]
-        t3 = [wide("t3", h) for h in halves]
-        t4 = [wide("t4", h) for h in halves]
-        result = [wide("result", h) for h in halves]
-        for h in halves:
-            nc.vector.tensor_tensor(grouped(t0[h][:]), grouped(curve[h][:]), spread(coef[h][:, 0, :]), ALU.subtract)
-        for h in halves:
-            nc.vector.tensor_tensor(grouped(t2[h][:]), grouped(nq[h][:]), spread(coef[h][:, 1, :]), ALU.mult)
-        for h in halves:
-            nc.vector.tensor_tensor(t1[h][:], na[h][:], t0[h][:], ALU.mult)
-        for h in halves:
-            nc.vector.tensor_tensor(t3[h][:], t2[h][:], t1[h][:], ALU.subtract)
-        for h in halves:
-            nc.vector.tensor_tensor(grouped(t4[h][:]), grouped(t3[h][:]), spread(weight[h][:]), ALU.mult)
-        for h in halves:
+            nc.scalar.activation(weight[h][:], e[h][:], ACT.Square, scale=2.0)
+
+        def step_factor(h):
+            nc.vector.tensor_tensor(factor[h][:, HG:], factor[h][:, :HG], weight[h][:], ALU.mult)
+
+        def step_coef(h):
+            nc.vector.tensor_tensor(coef[h][:], sums[h][:], factor[h][:], ALU.mult)
+
+        def step_t0(h):
+            nc.vector.tensor_tensor(grouped(t0[h][:]), grouped(curve[h][:]), spread(coef[h][:, :HG]), ALU.subtract)
+
+        def step_t2(h):
+            nc.vector.tensor_tensor(grouped(t2[h][:]), grouped(nq[h][:]), spread(coef[h][:, HG:]), ALU.mult)
+
+        def step_t1(h):
+            nc.vector.tensor_tensor(t1[h][:], wa[h][:], t0[h][:], ALU.mult)
+
+        def step_shifted(h):
             cols = slice(h * HJ, (h + 1) * HJ)
-            nc.vector.scalar_tensor_tensor(result[h][:], t4[h][:], gain[:], base_sb[:, cols], ALU.mult, ALU.add)
+            nc.vector.scalar_tensor_tensor(shifted[h][:], t2[h][:], gain[:], base_sb[:, cols], ALU.mult, ALU.add)
+
+        def step_result(h):
+            cols = slice(h * HJ, (h + 1) * HJ)
+            nc.vector.scalar_tensor_tensor(result[h][:], t1[h][:], neg_gain[:], shifted[h][:], ALU.mult, ALU.add)
             nc.sync.dma_start(out=out[:, cols], in_=result[h][:])
+
+        step_z(0)
+        step_ph(0)
+        step_nq(0)
+        step_rz(0)
+        step_ph_sum(0)
+        step_z(1)
+        step_ph(1)
+        step_mean(0)
+        step_nq(1)
+        step_rz(1)
+        step_d(0)
+        step_ph_sum(1)
+        step_npu(0)
+        step_c0(0)
+        step_ndq(0)
+        step_mean(1)
+        step_npu(1)
+        step_e(0)
+        step_e(1)
+        step_na(0)
+        step_d(1)
+        step_bend(0)
+        step_aq(0)
+        step_ndq(1)
+        step_tilt(0)
+        step_factor(0)
+        step_factor(1)
+        step_aq_sum(0)
+        step_na(1)
+        step_wa(0)
+        step_wa(1)
+        step_a_sq_sum(0)
+        step_curve(0)
+        step_aq(1)
+        step_tilt(1)
+        step_coef(0)
+        step_aq_sum(1)
+        step_bend(1)
+        step_t0(0)
+        step_a_sq_sum(1)
+        step_t2(0)
+        step_curve(1)
+        step_coef(1)
+        step_t1(0)
+        step_shifted(0)
+        step_t0(1)
+        step_t2(1)
+        step_result(0)
+        step_t1(1)
+        step_shifted(1)
+        step_result(1)

@@ -110,8 +110,23 @@ def tile_attend_gpgroupvote_kernel(tc, tab_words, tab_scales, w1, steep, wo, dy,
         nq, npu, d, ndq, na = (per_half(name, HJ) for name in ("nq", "npu", "d", "ndq", "na"))
         a_sq, tilt, aq, bend, curve = (per_half(name, HJ) for name in ("a_sq", "tilt", "aq", "bend", "curve"))
         t0, t1, t2, shifted, result, wa = (per_half(name, HJ) for name in ("t0", "t1", "t2", "shifted", "result", "wa"))
-        z, rz, ph_sum, mean, e, weight = (per_half(name, HG) for name in ("z", "rz", "ph_sum", "mean", "e", "weight"))
-        sums, factor, coef = (per_half(name, 2 * HG) for name in ("sums", "factor", "coef"))
+        z, ph_sum, mean = (per_half(name, HG) for name in ("z", "ph_sum", "mean"))
+        sums, coef = (per_half(name, 2 * HG) for name in ("sums", "coef"))
+        rz = keep.tile([P, G], F32, align_bytes=64)
+        e = keep.tile([P, G], F32, align_bytes=64)
+        weight = keep.tile([P, G], F32, align_bytes=64)
+        factor = keep.tile([P, 2, G], F32, align_bytes=64)
+        groups = [slice(h * HG, (h + 1) * HG) for h in halves]
+
+        def per_group(dst, src, scale, bias):
+            for g in range(HG):
+                cols = slice(g * GROUP, (g + 1) * GROUP)
+                if bias is None:
+                    nc.scalar.activation(dst[:, cols], src[:, cols], ACT.Copy, scale=scale[:, g : g + 1])
+                elif scale is None:
+                    nc.scalar.activation(dst[:, cols], src[:, cols], ACT.Identity, bias=bias[:, g : g + 1])
+                else:
+                    nc.scalar.activation(dst[:, cols], src[:, cols], ACT.Identity, bias=bias[:, g : g + 1], scale=scale[:, g : g + 1])
 
         for h in halves:
             nc.scalar.activation(p[h][:], a[h][:], ACT.Sigmoid, scale=s[:])
@@ -142,17 +157,20 @@ def tile_attend_gpgroupvote_kernel(tc, tab_words, tab_scales, w1, steep, wo, dy,
             nc.vector.scalar_tensor_tensor(nq[h][:], p[h][:], 1.0, p[h][:], ALU.subtract, ALU.mult)
 
         def step_rz(h):
-            nc.vector.reciprocal(rz[h][:], z[h][:])
-            nc.scalar.activation(factor[h][:, :HG], rz[h][:], ACT.Copy, scale=s_half[:])
+            nc.vector.reciprocal(rz[:, groups[h]], z[h][:])
+            nc.scalar.activation(factor[:, 0, groups[h]], rz[:, groups[h]], ACT.Copy, scale=s_half[:])
 
         def step_ph_sum(h):
             nc.vector.tensor_reduce(ph_sum[h][:], grouped(ph[h][:]), AXIS_X, ALU.add)
 
         def step_mean(h):
-            nc.vector.tensor_tensor(mean[h][:], ph_sum[h][:], rz[h][:], ALU.mult)
+            nc.vector.scalar_tensor_tensor(mean[h][:], ph_sum[h][:], -1.0, rz[:, groups[h]], ALU.mult, ALU.mult)
 
         def step_d(h):
-            nc.vector.tensor_tensor(grouped(d[h][:]), grouped(h1[h][:]), spread(mean[h][:]), ALU.subtract)
+            nc.vector.tensor_tensor(grouped(d[h][:]), grouped(h1[h][:]), spread(mean[h][:]), ALU.add)
+
+        def step_d_act(h):
+            per_group(d[h], h1[h], None, mean[h])
 
         def step_npu(h):
             nc.vector.scalar_tensor_tensor(npu[h][:], h_sq[h][:], 1.0, p[h][:], ALU.subtract, ALU.mult)
@@ -165,15 +183,16 @@ def tile_attend_gpgroupvote_kernel(tc, tab_words, tab_scales, w1, steep, wo, dy,
             nc.scalar.activation(a_sq[h][:], na[h][:], ACT.Square)
 
         def step_wa(h):
-            for g in range(HG):
-                cols = slice(g * GROUP, (g + 1) * GROUP)
-                nc.scalar.activation(wa[h][:, cols], na[h][:, cols], ACT.Copy, scale=weight[h][:, g : g + 1])
+            per_group(wa[h], na[h], weight[:, groups[h]], None)
+
+        def step_t0_act(h):
+            per_group(t0[h], curve[h], weight[:, groups[h]], coef[h][:, :HG])
 
         def step_bend(h):
             nc.vector.scalar_tensor_tensor(bend[h][:], h1[h][:], s_half[:], npu[h][:], ALU.subtract, ALU.mult)
 
         def step_aq(h):
-            nc.vector.tensor_tensor(aq[h][:], na[h][:], nq[h][:], ALU.mult)
+            nc.vector.scalar_tensor_tensor(aq[h][:], na[h][:], -1.0, nq[h][:], ALU.mult, ALU.mult)
 
         def step_tilt(h):
             nc.vector.scalar_tensor_tensor(tilt[h][:], p[h][:], 0.5, na[h][:], ALU.subtract, ALU.mult)
@@ -201,23 +220,36 @@ def tile_attend_gpgroupvote_kernel(tc, tab_words, tab_scales, w1, steep, wo, dy,
             )
 
         def step_e(h):
-            nc.vector.tensor_tensor(e[h][:], c0[:, h * HG : (h + 1) * HG], rz[h][:], ALU.mult)
-            nc.scalar.activation(weight[h][:], e[h][:], ACT.Square, scale=2.0)
+            nc.vector.tensor_tensor(e[:], c0[:], rz[:], ALU.mult)
+            nc.scalar.activation(weight[:], e[:], ACT.Square, scale=2.0)
 
         def step_factor(h):
-            nc.vector.tensor_tensor(factor[h][:, HG:], factor[h][:, :HG], weight[h][:], ALU.mult)
+            nc.vector.tensor_tensor(factor[:, 1, :], factor[:, 0, :], weight[:], ALU.mult)
 
         def step_coef(h):
-            nc.vector.tensor_tensor(coef[h][:], sums[h][:], factor[h][:], ALU.mult)
+            nc.vector.tensor_tensor(
+                coef[h][:].rearrange("p (k g) -> p k g", k=2), sums[h][:].rearrange("p (k g) -> p k g", k=2), factor[:, :, groups[h]], ALU.mult
+            )
+
+        def step_coef_w(h):
+            nc.vector.tensor_tensor(
+                coef[h][:].rearrange("p (k g) -> p k g", k=2),
+                sums[h][:].rearrange("p (k g) -> p k g", k=2),
+                factor[:, 1:2, groups[h]].to_broadcast([P, 2, HG]),
+                ALU.mult,
+            )
 
         def step_t0(h):
-            nc.vector.tensor_tensor(grouped(t0[h][:]), grouped(curve[h][:]), spread(coef[h][:, :HG]), ALU.subtract)
+            nc.vector.tensor_tensor(grouped(t0[h][:]), grouped(curve[h][:]), spread(coef[h][:, :HG]), ALU.add)
 
         def step_t2(h):
             nc.vector.tensor_tensor(grouped(t2[h][:]), grouped(nq[h][:]), spread(coef[h][:, HG:]), ALU.mult)
 
         def step_t1(h):
             nc.vector.tensor_tensor(t1[h][:], wa[h][:], t0[h][:], ALU.mult)
+
+        def step_t1_w(h):
+            nc.vector.tensor_tensor(t1[h][:], na[h][:], t0[h][:], ALU.mult)
 
         def step_shifted(h):
             cols = slice(h * HJ, (h + 1) * HJ)
@@ -236,46 +268,44 @@ def tile_attend_gpgroupvote_kernel(tc, tab_words, tab_scales, w1, steep, wo, dy,
         step_z(1)
         step_ph(1)
         step_mean(0)
-        step_nq(1)
         step_rz(1)
-        step_d(0)
         step_ph_sum(1)
         step_npu(0)
-        step_c0(0)
-        step_ndq(0)
+        step_nq(1)
         step_mean(1)
+        step_c0(0)
+        step_d_act(0)
         step_npu(1)
-        step_e(0)
-        step_e(1)
-        step_na(0)
         step_d(1)
         step_bend(0)
-        step_aq(0)
+        step_e(0)
+        step_ndq(0)
         step_ndq(1)
-        step_tilt(0)
-        step_factor(0)
-        step_factor(1)
-        step_aq_sum(0)
+        step_bend(1)
+        step_na(0)
         step_na(1)
         step_wa(0)
         step_wa(1)
-        step_a_sq_sum(0)
-        step_curve(0)
+        step_factor(0)
+        step_aq(0)
         step_aq(1)
+        step_tilt(0)
         step_tilt(1)
-        step_coef(0)
+        step_aq_sum(0)
         step_aq_sum(1)
-        step_bend(1)
-        step_t0(0)
+        step_a_sq_sum(0)
         step_a_sq_sum(1)
-        step_t2(0)
+        step_curve(0)
+        step_coef(0)
         step_curve(1)
         step_coef(1)
-        step_t1(0)
-        step_shifted(0)
+        step_t0(0)
+        step_t2(0)
         step_t0(1)
         step_t2(1)
-        step_result(0)
-        step_t1(1)
+        step_t1(0)
+        step_shifted(0)
         step_shifted(1)
+        step_t1(1)
+        step_result(0)
         step_result(1)

from contextlib import ExitStack

import concourse.mybir as mybir

K, R, F, T, J, G = 512, 128, 512, 2048, 512, 64
FLOPS = 2 * K * R * J + 2 * F * R * G

F32 = mybir.dt.float32
BF16 = mybir.dt.bfloat16
I32 = mybir.dt.int32
U32 = mybir.dt.uint32
U16 = mybir.dt.uint16
U8 = mybir.dt.uint8
FP8X4 = mybir.dt.float8_e4m3fn_x4
FP4X4 = mybir.dt.float4_e2m1fn_x4
ACT = mybir.ActivationFunctionType
ALU = mybir.AluOpType
AXIS_X = mybir.AxisListType.X

P = 128
PACK = 4
GROUP = J // G
HALVES = 2
HJ = J // HALVES
HG = G // HALVES


def grouped(ap):
    return ap.rearrange("p (g i) -> p g i", i=GROUP)


def spread(ap):
    return ap.rearrange("p (g o) -> p g o", o=1).to_broadcast([P, HG, GROUP])


def tile_attend_gpgroupvote_kernel(tc, tab_words, tab_scales, w1, steep, wo, dy, og, base, offs, out):
    nc = tc.nc
    with ExitStack() as ctx:
        keep = ctx.enter_context(tc.tile_pool(name="keep", bufs=1))
        psum = ctx.enter_context(tc.psum_pool(name="psum", bufs=1))

        halves = range(HALVES)

        def per_half(name, width):
            return [keep.tile([P, width], F32, name=f"{name}{h}", align_bytes=64) for h in halves]

        offsets = keep.tile([P, J // 16], U16)
        nc.sync.dma_start(offsets[:], offs)
        s = keep.tile([P, 1], F32)
        nc.scalar.dma_start(out=s[:], in_=steep)
        w1_raw = keep.tile([P, PACK, R], F32, tag="stage", align_bytes=64)
        nc.sync.dma_start(out=w1_raw[:], in_=w1.rearrange("(p t) r -> p t r", t=PACK))

        scale_window = keep.tile([P, T], U8, align_bytes=64)
        nc.vector.memset(scale_window[:].bitcast(I32), 0)
        for q in range(4):
            nc.sync.dma_start(
                out=scale_window[32 * q : 32 * q + 4, :].bitcast(I32),
                in_=tab_scales[0, 4 * q : 4 * q + 4, :].bitcast(I32),
            )
        word_window = keep.tile([P, T], U16, align_bytes=64)
        nc.sync.dma_start(out=word_window[:].bitcast(I32), in_=tab_words[0].bitcast(I32))
        gain = keep.tile([P, 1], F32)
        nc.sync.dma_start(out=gain[:], in_=og)

        warm_in = keep.tile([P, 1], F32)
        nc.gpsimd.memset(warm_in[:], 0.0)
        warm_out = keep.tile([P, 1], F32)
        nc.scalar.activation(warm_out[:], warm_in[:], ACT.Sigmoid)

        def interleave(dst, src):
            nc.scalar.copy(
                out=dst.rearrange("p (c i) t -> p c t i", i=4),
                in_=src.rearrange("p t (c i) -> p c t i", i=4),
            )

        def quantise(name, values, width):
            codes = keep.tile([P, width], U32, name=f"{name}_codes", align_bytes=64)
            scales = keep.tile([P, width], U8, name=f"{name}_scales", align_bytes=64)
            nc.vector.quantize_mx(out=codes[:].bitcast(FP8X4), scales=scales[:], in_=values.rearrange("p c t -> p (c t)"))
            return codes, scales

        w1_bf = keep.tile([P, R, PACK], BF16, align_bytes=64)
        interleave(w1_bf[:], w1_raw[:])
        s_half = keep.tile([P, 1], F32)
        nc.gpsimd.tensor_scalar(s_half[:], s[:], 0.5, 0.0, ALU.mult, ALU.add)
        neg_gain = keep.tile([P, 1], F32)
        nc.gpsimd.tensor_scalar(neg_gain[:], gain[:], -1.0, 0.0, ALU.mult, ALU.add)

        lists = [offsets[:, h * (HJ // 16) : (h + 1) * (HJ // 16)] for h in halves]
        tab_s = [keep.tile([P, HJ], U8, name=f"tab_s{h}", align_bytes=64) for h in halves]
        tab_w = [keep.tile([P, HJ], U16, name=f"tab_w{h}", align_bytes=64) for h in halves]
        for h in halves:
            nc.vector.tensor_copy(tab_s[h][:], scale_window[:].indirect(lists[h]))
        w1_codes, w1_scales = quantise("w1", w1_bf[:], R)
        a = [psum.tile([P, HJ], F32, name=f"a{h}") for h in halves]
        for h in halves:
            nc.vector.tensor_copy(tab_w[h][:], word_window[:].indirect(lists[h]))
            nc.tensor.matmul_mx(
                out=a[h][:],
                lhsT=w1_codes[:].bitcast(FP8X4),
                lhsT_scale=w1_scales[:],
                rhs=tab_w[h][:].bitcast(FP4X4),
                rhs_scale=tab_s[h][:],
                start=True,
                stop=True,
            )

        p, h1, h_sq, ph = (per_half(name, HJ) for name in ("p", "h1", "h_sq", "ph"))
        nq, npu, d, ndq, na = (per_half(name, HJ) for name in ("nq", "npu", "d", "ndq", "na"))
        a_sq, tilt, aq, bend, curve = (per_half(name, HJ) for name in ("a_sq", "tilt", "aq", "bend", "curve"))
        t0, t1, t2, shifted, result, wa = (per_half(name, HJ) for name in ("t0", "t1", "t2", "shifted", "result", "wa"))
        z, ph_sum, mean = (per_half(name, HG) for name in ("z", "ph_sum", "mean"))
        sums, coef = (per_half(name, 2 * HG) for name in ("sums", "coef"))
        rz = keep.tile([P, G], F32, align_bytes=64)
        e = keep.tile([P, G], F32, align_bytes=64)
        weight = keep.tile([P, G], F32, align_bytes=64)
        factor = keep.tile([P, 2, G], F32, align_bytes=64)
        groups = [slice(h * HG, (h + 1) * HG) for h in halves]

        def per_group(dst, src, scale, bias):
            for g in range(HG):
                cols = slice(g * GROUP, (g + 1) * GROUP)
                if bias is None:
                    nc.scalar.activation(dst[:, cols], src[:, cols], ACT.Copy, scale=scale[:, g : g + 1])
                elif scale is None:
                    nc.scalar.activation(dst[:, cols], src[:, cols], ACT.Identity, bias=bias[:, g : g + 1])
                else:
                    nc.scalar.activation(dst[:, cols], src[:, cols], ACT.Identity, bias=bias[:, g : g + 1], scale=scale[:, g : g + 1])

        for h in halves:
            nc.scalar.activation(p[h][:], a[h][:], ACT.Sigmoid, scale=s[:])
            nc.scalar.activation(h1[h][:], a[h][:], ACT.Tanh)
        for h in halves:
            nc.scalar.activation(h_sq[h][:], h1[h][:], ACT.Square)

        last_raw = keep.tile([P, PACK * (R + G)], F32, tag="stage", align_bytes=64)
        wo_raw = last_raw[:, : PACK * R].rearrange("p (t r) -> p t r", t=PACK)
        dy_raw = last_raw[:, PACK * R :].rearrange("p (t g) -> p t g", t=PACK)
        nc.sync.dma_start(out=wo_raw, in_=wo.rearrange("(p t) r -> p t r", t=PACK))
        nc.sync.dma_start(out=dy_raw, in_=dy.rearrange("(p t) g -> p t g", t=PACK))
        wo_bf = keep.tile([P, R, PACK], BF16, align_bytes=64)
        dy_bf = keep.tile([P, G, PACK], BF16, align_bytes=64)
        interleave(wo_bf[:], wo_raw)
        interleave(dy_bf[:], dy_raw)
        base_sb = keep.tile([P, J], F32, tag="stage", align_bytes=64)
        nc.sync.dma_start(out=base_sb[:], in_=base)
        c0 = psum.tile([P, G], F32)

        def step_z(h):
            nc.vector.tensor_reduce(z[h][:], grouped(p[h][:]), AXIS_X, ALU.add)

        def step_ph(h):
            nc.vector.tensor_tensor(ph[h][:], p[h][:], h1[h][:], ALU.mult)

        def step_nq(h):
            nc.vector.scalar_tensor_tensor(nq[h][:], p[h][:], 1.0, p[h][:], ALU.subtract, ALU.mult)

        def step_rz(h):
            nc.vector.reciprocal(rz[:, groups[h]], z[h][:])
            nc.scalar.activation(factor[:, 0, groups[h]], rz[:, groups[h]], ACT.Copy, scale=s_half[:])

        def step_ph_sum(h):
            nc.vector.tensor_reduce(ph_sum[h][:], grouped(ph[h][:]), AXIS_X, ALU.add)

        def step_mean(h):
            nc.vector.scalar_tensor_tensor(mean[h][:], ph_sum[h][:], -1.0, rz[:, groups[h]], ALU.mult, ALU.mult)

        def step_d(h):
            nc.vector.tensor_tensor(grouped(d[h][:]), grouped(h1[h][:]), spread(mean[h][:]), ALU.add)

        def step_d_act(h):
            per_group(d[h], h1[h], None, mean[h])

        def step_npu(h):
            nc.vector.scalar_tensor_tensor(npu[h][:], h_sq[h][:], 1.0, p[h][:], ALU.subtract, ALU.mult)

        def step_ndq(h):
            nc.vector.scalar_tensor_tensor(ndq[h][:], d[h][:], s[:], nq[h][:], ALU.mult, ALU.mult)

        def step_na(h):
            nc.vector.tensor_tensor(na[h][:], ndq[h][:], npu[h][:], ALU.add)
            nc.scalar.activation(a_sq[h][:], na[h][:], ACT.Square)

        def step_wa(h):
            per_group(wa[h], na[h], weight[:, groups[h]], None)

        def step_t0_act(h):
            per_group(t0[h], curve[h], weight[:, groups[h]], coef[h][:, :HG])

        def step_bend(h):
            nc.vector.scalar_tensor_tensor(bend[h][:], h1[h][:], s_half[:], npu[h][:], ALU.subtract, ALU.mult)

        def step_aq(h):
            nc.vector.scalar_tensor_tensor(aq[h][:], na[h][:], -1.0, nq[h][:], ALU.mult, ALU.mult)

        def step_tilt(h):
            nc.vector.scalar_tensor_tensor(tilt[h][:], p[h][:], 0.5, na[h][:], ALU.subtract, ALU.mult)

        def step_aq_sum(h):
            nc.vector.tensor_reduce(sums[h][:, :HG], grouped(aq[h][:]), AXIS_X, ALU.add)

        def step_a_sq_sum(h):
            nc.vector.tensor_reduce(sums[h][:, HG:], grouped(a_sq[h][:]), AXIS_X, ALU.add)

        def step_curve(h):
            nc.vector.scalar_tensor_tensor(curve[h][:], tilt[h][:], s[:], bend[h][:], ALU.mult, ALU.add)

        def step_c0(h):
            wo_codes, wo_scales = quantise("wo", wo_bf[:], R)
            dy_codes, dy_scales = quantise("dy", dy_bf[:], G)
            nc.tensor.matmul_mx(
                out=c0[:],
                lhsT=wo_codes[:].bitcast(FP8X4),
                lhsT_scale=wo_scales[:],
                rhs=dy_codes[:].bitcast(FP8X4),
                rhs_scale=dy_scales[:],
                start=True,
                stop=True,
            )

        def step_e(h):
            nc.vector.tensor_tensor(e[:], c0[:], rz[:], ALU.mult)
            nc.scalar.activation(weight[:], e[:], ACT.Square, scale=2.0)

        def step_factor(h):
            nc.vector.tensor_tensor(factor[:, 1, :], factor[:, 0, :], weight[:], ALU.mult)

        def step_coef(h):
            nc.vector.tensor_tensor(
                coef[h][:].rearrange("p (k g) -> p k g", k=2), sums[h][:].rearrange("p (k g) -> p k g", k=2), factor[:, :, groups[h]], ALU.mult
            )

        def step_coef_w(h):
            nc.vector.tensor_tensor(
                coef[h][:].rearrange("p (k g) -> p k g", k=2),
                sums[h][:].rearrange("p (k g) -> p k g", k=2),
                factor[:, 1:2, groups[h]].to_broadcast([P, 2, HG]),
                ALU.mult,
            )

        def step_t0(h):
            nc.vector.tensor_tensor(grouped(t0[h][:]), grouped(curve[h][:]), spread(coef[h][:, :HG]), ALU.add)

        def step_t2(h):
            nc.vector.tensor_tensor(grouped(t2[h][:]), grouped(nq[h][:]), spread(coef[h][:, HG:]), ALU.mult)

        def step_t1(h):
            nc.vector.tensor_tensor(t1[h][:], wa[h][:], t0[h][:], ALU.mult)

        def step_t1_w(h):
            nc.vector.tensor_tensor(t1[h][:], na[h][:], t0[h][:], ALU.mult)

        def step_shifted(h):
            cols = slice(h * HJ, (h + 1) * HJ)
            nc.vector.scalar_tensor_tensor(shifted[h][:], t2[h][:], gain[:], base_sb[:, cols], ALU.mult, ALU.add)

        def step_result(h):
            cols = slice(h * HJ, (h + 1) * HJ)
            nc.vector.scalar_tensor_tensor(result[h][:], t1[h][:], neg_gain[:], shifted[h][:], ALU.mult, ALU.add)
            nc.sync.dma_start(out=out[:, cols], in_=result[h][:])

        step_z(0)
        step_ph(0)
        step_nq(0)
        step_rz(0)
        step_ph_sum(0)
        step_z(1)
        step_ph(1)
        step_mean(0)
        step_rz(1)
        step_ph_sum(1)
        step_npu(0)
        step_nq(1)
        step_mean(1)
        step_c0(0)
        step_d_act(0)
        step_npu(1)
        step_d(1)
        step_bend(0)
        step_e(0)
        step_ndq(0)
        step_ndq(1)
        step_bend(1)
        step_na(0)
        step_na(1)
        step_wa(0)
        step_wa(1)
        step_factor(0)
        step_aq(0)
        step_aq(1)
        step_tilt(0)
        step_tilt(1)
        step_aq_sum(0)
        step_aq_sum(1)
        step_a_sq_sum(0)
        step_a_sq_sum(1)
        step_curve(0)
        step_coef(0)
        step_curve(1)
        step_coef(1)
        step_t0(0)
        step_t2(0)
        step_t0(1)
        step_t2(1)
        step_t1(0)
        step_shifted(0)
        step_shifted(1)
        step_t1(1)
        step_result(0)
        step_result(1)
